import numpy as np
import ml_dtypes


def mxq(x, axis, fmt="e4m3"):
    dtype, down = {"e4m3": (ml_dtypes.float8_e4m3fn, 7), "e5m2": (ml_dtypes.float8_e5m2, 14)}[fmt]
    v = np.moveaxis(np.asarray(x, np.float32).astype(ml_dtypes.bfloat16).astype(np.float64), axis, -1)
    blocks = v.reshape(v.shape[:-1] + (-1, 32))
    amax = np.abs(blocks).max(-1, keepdims=True)
    byte = np.maximum(np.where(amax > 0, np.frexp(amax)[1] - 1 + 127, 0) - down, 1)
    scale = np.exp2(byte - 127.0)
    codes = (blocks / scale).astype(np.float32).astype(dtype).astype(np.float64)
    return np.moveaxis((codes * scale).reshape(v.shape), -1, axis)


WIDE = False


def mx_kscale(k):
    if not WIDE:
        return np.ones(k)
    levels = np.array([30, -30])
    if k % 512:
        return np.exp2(np.random.permutation(np.resize(levels, k // 32))).repeat(32)
    a = np.empty((k // 512, 16))
    for p in range(k // 512):
        a[p, :8] = np.random.permutation(np.resize(levels, 8))
        for g in range(8):
            far = levels[np.abs(levels - a[p, g]) >= 10]
            a[p, g + 8] = far[np.random.randint(len(far))]
    return np.exp2(a.ravel()).repeat(32)


def f64(x):
    return np.asarray(x).astype(np.float64)


def striped(idx):
    return np.tile(np.asarray(idx).reshape(-1, 16).T, (8, 1)).astype(np.uint16)


def unstriped(offs):
    return offs[:16].T.reshape(-1).astype(np.int64)


E2M1 = np.array([0.0, 0.5, 1.0, 1.5, 2.0, 3.0, 4.0, 6.0, -0.0, -0.5, -1.0, -1.5, -2.0, -3.0, -4.0, -6.0])


def pack_weight(w, fmt):
    k, n = w.shape
    w = f64(np.asarray(w, np.float32).astype(ml_dtypes.bfloat16)).reshape(k // 32, 32, n)
    amax = np.abs(w).max(1)
    if fmt in ("e4m3", "e5m2"):
        byte = np.frexp(amax)[1] - 1 + 127 - (7 if fmt == "e4m3" else 14)
    else:
        mant, ex = np.frexp(amax / 6.0)
        byte = np.where(mant > 0.5, ex, ex - 1) + 127
    byte = np.clip(np.where(amax > 0, byte, 1), 1, 254)
    scaled = (w * np.exp2(127.0 - byte)[:, None, :]).reshape(k, n).astype(np.float32)
    by_word = np.ascontiguousarray(scaled.reshape(k // 512, 128, 4, n).transpose(0, 1, 3, 2))
    if fmt in ("e4m3", "e5m2"):
        words = by_word.astype(ml_dtypes.float8_e4m3fn if fmt == "e4m3" else ml_dtypes.float8_e5m2).view(np.uint8)
    else:
        c = by_word.astype(ml_dtypes.float4_e2m1fn).view(np.uint8) & 0xF
        words = (c[..., 0::2] | (c[..., 1::2] << 4)).reshape(k // 512, 128, 2 * n)
    return np.ascontiguousarray(words), np.ascontiguousarray(byte.astype(np.uint8).reshape(k // 512, 16, n))


def unpack_weight(words, scales, fmt):
    g, _, n = scales.shape
    words = np.ascontiguousarray(words).reshape(g, 128, n, -1)
    if fmt in ("e4m3", "e5m2"):
        vals = words.view(ml_dtypes.float8_e4m3fn if fmt == "e4m3" else ml_dtypes.float8_e5m2).astype(np.float64)
    else:
        nib = np.empty((g, 128, n, 4), np.uint8)
        nib[..., 0::2] = words & 0xF
        nib[..., 1::2] = words >> 4
        vals = E2M1[nib]
    vals = vals * np.repeat(np.exp2(scales.astype(np.float64) - 127.0), 8, axis=1)[..., None]
    return vals.transpose(0, 1, 3, 2).reshape(g * 512, n)


K, T, J, R, F, Z, X, V, O, N, E = 512, 1024, 256, 512, 512, 1024, 512, 512, 128, 256, 512


def setup_inputs():
    n = np.random.standard_normal
    idx = np.random.permutation(T)[:J]
    idx2 = np.random.permutation(Z)[:J]
    idx3 = np.random.permutation(X)[:O]
    idx4 = np.random.permutation(V)[:O]
    idx5 = np.random.permutation(J)[:O]
    idx6 = np.random.permutation(E)[:O]
    idx7 = np.random.permutation(E)[:O]
    fk = mx_kscale(K)
    ff = mx_kscale(F)
    fr = mx_kscale(R)
    xtp = pack_weight(n((K, T)) / fk[:, None], "e5m2")
    xop = pack_weight(n((F, Z)) / ff[:, None], "e4m3")
    wp = pack_weight(n((K, R)) * 1 / np.sqrt(K) * fk[:, None] * fr, "e2m1")
    w0p = pack_weight(n((F, R)) * 1 / np.sqrt(F) * ff[:, None] * fr, "e2m1")
    wbp = pack_weight(n((R, N)) * 1 / np.sqrt(R) / fr[:, None], "e2m1")
    return {
        "xt_words": xtp[0],
        "xt_scales": xtp[1],
        "xo_words": xop[0],
        "xo_scales": xop[1],
        "w_words": wp[0],
        "w_scales": wp[1],
        "w0_words": w0p[0],
        "w0_scales": w0p[1],
        "tb": (n((R, X)) * 0.9).astype(np.float32),
        "tc2": (n((R, V)) * 0.9).astype(np.float32),
        "wb_words": wbp[0],
        "wb_scales": wbp[1],
        "offs": striped(idx),
        "offs2": striped(idx2),
        "offs3": striped(idx3),
        "offs4": striped(idx4),
        "offs5": striped(idx5),
        "offs6": striped(idx6),
        "offs7": striped(idx7),
    }


def reference(xt_words, xt_scales, xo_words, xo_scales, w_words, w_scales, w0_words, w0_scales, tb, tc2, wb_words, wb_scales, offs, offs2, offs3, offs4, offs5, offs6, offs7):
    idx = unstriped(offs)
    idx2 = unstriped(offs2)
    idx3 = unstriped(offs3)
    idx4 = unstriped(offs4)
    idx5 = unstriped(offs5)
    idx6 = unstriped(offs6)
    idx7 = unstriped(offs7)
    xtu = unpack_weight(xt_words, xt_scales, "e5m2")
    xou = unpack_weight(xo_words, xo_scales, "e4m3")
    wu = unpack_weight(w_words, w_scales, "e2m1")
    w0u = unpack_weight(w0_words, w0_scales, "e2m1")
    wbu = unpack_weight(wb_words, wb_scales, "e2m1")
    xtidxg = xtu[:, idx]
    xoidx2g = xou[:, idx2]
    a = wu.T @ xtidxg + w0u.T @ xoidx2g
    la = a[:, 0:1]
    la2 = a[:, 128:129]
    hid = np.maximum(f64(tb)[:, idx3] * la, f64(tc2)[:, idx4] * la2) - a[:, idx5]
    hidq = mxq(hid, 0, "e4m3")
    p = wbu.T @ hidq
    pa = np.zeros((N, E))
    pa[:, idx6] = p
    pb = np.zeros((N, E))
    pb[:, idx7] = p
    y = pa + pb
    return y

@@ -1,0 +1,179 @@
+from contextlib import ExitStack
+
+import concourse.mybir as mybir
+
+F32 = mybir.dt.float32
+BF16 = mybir.dt.bfloat16
+I32 = mybir.dt.int32
+U32 = mybir.dt.uint32
+U16 = mybir.dt.uint16
+U8 = mybir.dt.uint8
+E4M3 = mybir.dt.float8_e4m3fn_x4
+E5M2 = mybir.dt.float8_e5m2_x4
+E2M1 = mybir.dt.float4_e2m1fn_x4
+ALU = mybir.AluOpType
+COPY = mybir.ActivationFunctionType.Copy
+
+P = 128
+PACK = 4
+T, J, R, X, O, N, E = 1024, 256, 512, 512, 128, 256, 512
+FLOPS = 2 * (2 * 512 * R * J + R * N * O)
+
+
+def tile_list_twotables_bank_one_pagetwice_kernel(
+    tc, xt_words, xt_scales, xo_words, xo_scales, w_words, w_scales, w0_words, w0_scales,
+    tb, tc2, wb_words, wb_scales, offs, offs2, offs3, offs4, offs5, offs6, offs7, out,
+):
+    nc = tc.nc
+    with ExitStack() as ctx:
+        sb = ctx.enter_context(tc.tile_pool(name="sb", bufs=1))
+        ps = ctx.enter_context(tc.psum_pool(name="ps", bufs=1))
+
+        def tile(name, shape, dtype):
+            return sb.tile(shape, dtype, name=name, align_bytes=64)
+
+        def load_list(name, src):
+            t = tile(name, list(src.shape), U16)
+            nc.sync.dma_start(t[:], src)
+            return t
+
+        def load_plane(queue, plane, src):
+            for q in range(4):
+                queue.dma_start(plane[32 * q : 32 * q + 4, :].bitcast(I32), src[0, 4 * q : 4 * q + 4, :].bitcast(I32))
+
+        def load_halves(stage, src):
+            rows = src[0].rearrange("(h q r) n -> q r h n", h=2, q=2, r=4)
+            for q in range(2):
+                nc.gpsimd.dma_start(stage[32 * q : 32 * q + 4, :, :].bitcast(I32), rows[q].bitcast(I32))
+
+        xt_plane = tile("xt_plane", [P, T], U8)
+        xo_plane = tile("xo_plane", [P, T], U8)
+        w_stage = tile("w_stage", [P, 2, R], U8)
+        w0_stage = tile("w0_stage", [P, 2, R], U8)
+        wb_plane = tile("wb_plane", [P, N], U8)
+        nc.vector.memset(xt_plane[:].bitcast(I32), 0)
+        nc.vector.memset(w_stage[:].bitcast(I32), 0)
+        nc.vector.memset(w0_stage[:].bitcast(I32), 0)
+        nc.vector.memset(xo_plane[:].bitcast(I32), 0)
+        nc.vector.memset(wb_plane[:].bitcast(I32), 0)
+        pages = [[tile(f"page{s}{h}", [P, E], F32) for h in range(2)] for s in range(2)]
+        for s in range(2):
+            for h in range(2):
+                nc.vector.memset(pages[s][h][:], 0.0)
+
+        xt_sb = tile("xt_sb", [P, T], U32)
+        xo_sb = tile("xo_sb", [P, T], U32)
+        w_sb = tile("w_sb", [P, 2 * R], U8)
+        w0_sb = tile("w0_sb", [P, 2 * R], U8)
+        wb_sb = tile("wb_sb", [P, 2 * N], U8)
+        tb_sb = [tile(f"tb{t}", [P, X], F32) for t in range(PACK)]
+        tc_sb = [tile(f"tc{t}", [P, X], F32) for t in range(PACK)]
+        tb_rows = tb.rearrange("(p t) x -> t p x", t=PACK)
+        tc_rows = tc2.rearrange("(p t) x -> t p x", t=PACK)
+
+        nc.sync.dma_start(xt_sb[:].bitcast(I32), xt_words[0].rearrange("p n t -> p (n t)").bitcast(I32))
+        l1 = load_list("l1", offs)
+        load_plane(nc.sync, xt_plane, xt_scales)
+        nc.sync.dma_start(w_sb[:].bitcast(I32), w_words[0].bitcast(I32))
+        nc.sync.dma_start(xo_sb[:].bitcast(I32), xo_words[0].rearrange("p n t -> p (n t)").bitcast(I32))
+        l2 = load_list("l2", offs2)
+        load_plane(nc.sync, xo_plane, xo_scales)
+        nc.sync.dma_start(w0_sb[:].bitcast(I32), w0_words[0].bitcast(I32))
+        load_halves(w_stage, w_scales)
+        load_halves(w0_stage, w0_scales)
+        nc.sync.dma_start(tb_sb[0][:], tb_rows[0])
+        nc.sync.dma_start(tc_sb[0][:], tc_rows[0])
+        l3 = load_list("l3", offs3)
+        l4 = load_list("l4", offs4)
+        nc.sync.dma_start(tb_sb[1][:], tb_rows[1])
+        l5 = load_list("l5", offs5)
+        nc.sync.dma_start(tc_sb[1][:], tc_rows[1])
+        for t in range(2, PACK):
+            nc.sync.dma_start(tb_sb[t][:], tb_rows[t])
+            nc.sync.dma_start(tc_sb[t][:], tc_rows[t])
+        nc.sync.dma_start(wb_sb[:].bitcast(I32), wb_words[0].bitcast(I32))
+        l6 = load_list("l6", offs6)
+        l7 = load_list("l7", offs7)
+        load_plane(nc.gpsimd, wb_plane, wb_scales)
+
+        def deal_weight(name, words, stage):
+            codes = tile(name + "_codes", [P, 2 * R], U8)
+            plane = tile(name + "_dealt", [P, R], U8)
+            nc.scalar.copy(
+                codes[:].bitcast(U16).rearrange("p (t c i) -> p c t i", t=PACK, i=8),
+                words[:].bitcast(U16).rearrange("p (c i t) -> p c t i", t=PACK, i=8),
+            )
+            nc.vector.tensor_copy(stage[64:128, 0, :].bitcast(I32), stage[0:64, 1, :].bitcast(I32))
+            nc.vector.tensor_copy(
+                plane[:].rearrange("p (t c i) -> p c t i", t=PACK, i=16),
+                stage[:, 0, :].rearrange("p (c i t) -> p c t i", t=PACK, i=16),
+            )
+            return codes, plane
+
+        def pick(name, words, plane, lst):
+            gw = tile(name + "_gw", [P, J], U32)
+            gs = tile(name + "_gs", [P, J], U8)
+            nc.vector.tensor_copy(gs[:], plane[:].indirect(lst[:]))
+            nc.vector.tensor_copy(gw[:], words[:].indirect(lst[:]))
+            return gw, gs
+
+        xt_gw, xt_gs = pick("xt", xt_sb, xt_plane, l1)
+        w_codes, w_plane = deal_weight("w", w_sb, w_stage)
+        banks = [ps.tile([P, J], F32, name=f"acc{t}") for t in range(PACK)]
+        for t in range(PACK):
+            nc.tensor.matmul_mx(
+                banks[t][:], lhsT=w_codes[:, 2 * P * t : 2 * P * (t + 1)].bitcast(E2M1), lhsT_scale=w_plane[:, P * t : P * (t + 1)],
+                rhs=xt_gw[:].bitcast(E5M2), rhs_scale=xt_gs[:], start=True, stop=False,
+            )
+        xo_gw, xo_gs = pick("xo", xo_sb, xo_plane, l2)
+        w0_codes, w0_plane = deal_weight("w0", w0_sb, w0_stage)
+        for t in range(PACK):
+            nc.tensor.matmul_mx(
+                banks[t][:], lhsT=w0_codes[:, 2 * P * t : 2 * P * (t + 1)].bitcast(E2M1), lhsT_scale=w0_plane[:, P * t : P * (t + 1)],
+                rhs=xo_gw[:].bitcast(E4M3), rhs_scale=xo_gs[:], start=False, stop=True,
+            )
+
+        a_sb = [tile(f"a{t}", [P, J], F32) for t in range(PACK)]
+        u = tile("u", [P, PACK, O], F32)
+        v = tile("v", [P, PACK, O], F32)
+        m = tile("m", [P, PACK, O], F32)
+        g = tile("g", [P, PACK, O], F32)
+        d = tile("d", [P, PACK, O], BF16)
+        for t in range(PACK):
+            if t < 2:
+                nc.vector.tensor_copy(a_sb[t][:], banks[t][:])
+            else:
+                nc.scalar.copy(a_sb[t][:], banks[t][:])
+            nc.scalar.activation(u[:, t, :], tb_sb[t][:].indirect(l3[:]), COPY, scale=a_sb[t][:, 0:1])
+            nc.scalar.activation(v[:, t, :], tc_sb[t][:].indirect(l4[:]), COPY, scale=a_sb[t][:, 128:129])
+            nc.vector.tensor_copy(g[:, t, :], a_sb[t][:].indirect(l5[:]))
+            nc.vector.tensor_tensor(m[:, t, :], u[:, t, :], v[:, t, :], ALU.max)
+            nc.vector.tensor_tensor(d[:, t, :], m[:, t, :], g[:, t, :], ALU.subtract)
+
+        hid = tile("hid", [P, O * PACK], BF16)
+        nc.vector.tensor_copy(
+            hid[:].rearrange("p (c i t) -> p c t i", t=PACK, i=4),
+            d[:].rearrange("p t (c i) -> p c t i", i=4),
+        )
+        hid_codes = tile("hid_codes", [P, O], U32)
+        hid_plane = tile("hid_plane", [P, O], U8)
+        nc.vector.quantize_mx(hid_codes[:].bitcast(E4M3), hid_plane[:], hid[:])
+
+        p_sb = [tile(f"p{h}", [P, O], F32) for h in range(2)]
+        for h in range(2):
+            acc = ps.tile([P, O], F32, name=f"pacc{h}")
+            nc.tensor.matmul_mx(
+                acc[:], lhsT=wb_sb[:, 2 * P * h : 2 * P * (h + 1)].bitcast(E2M1), lhsT_scale=wb_plane[:, P * h : P * (h + 1)],
+                rhs=hid_codes[:].bitcast(E4M3), rhs_scale=hid_plane[:], start=True, stop=True,
+            )
+            if h == 0:
+                nc.vector.tensor_copy(p_sb[h][:], acc[:])
+            else:
+                nc.scalar.copy(p_sb[h][:], acc[:])
+        for h in range(2):
+            nc.vector.tensor_copy(pages[0][h][:].indirect(l6[:]), p_sb[h][:])
+            nc.scalar.activation(pages[1][h][:].indirect(l7[:]), p_sb[h][:], COPY)
+        for h in range(2):
+            y = tile(f"y{h}", [P, E], F32)
+            nc.vector.tensor_tensor(y[:], pages[0][h][:], pages[1][h][:], ALU.add)
+            nc.sync.dma_start(out[P * h : P * (h + 1), :], y[:])

@@ -44,17 +44,15 @@ def tile_list_twotables_bank_one_pagetwice_kernel(
         def load_halves(stage, src):
             rows = src[0].rearrange("(h q r) n -> q r h n", h=2, q=2, r=4)
             for q in range(2):
-                nc.gpsimd.dma_start(stage[32 * q : 32 * q + 4, :, :].bitcast(I32), rows[q].bitcast(I32))
+                nc.sync.dma_start(stage[32 * q : 32 * q + 4].bitcast(I32), rows[q].bitcast(I32))
 
-        xt_plane = tile("xt_plane", [P, T], U8)
-        xo_plane = tile("xo_plane", [P, T], U8)
-        w_stage = tile("w_stage", [P, 2, R], U8)
-        w0_stage = tile("w0_stage", [P, 2, R], U8)
+        xt_stage = tile("xt_stage", [64, 2, T], U8)
+        xo_stage = tile("xo_stage", [64, 2, T], U8)
+        w_stage = tile("w_stage", [P, 2, 2 * R], U8)
         wb_plane = tile("wb_plane", [P, N], U8)
-        nc.vector.memset(xt_plane[:].bitcast(I32), 0)
-        nc.vector.memset(w_stage[:].bitcast(I32), 0)
-        nc.vector.memset(w0_stage[:].bitcast(I32), 0)
-        nc.vector.memset(xo_plane[:].bitcast(I32), 0)
+        nc.vector.memset(xt_stage[:].bitcast(I32), 0)
+        nc.vector.memset(xo_stage[:].bitcast(I32), 0)
+        nc.vector.memset(w_stage[0:64].bitcast(I32), 0)
         nc.vector.memset(wb_plane[:].bitcast(I32), 0)
         pages = [[tile(f"page{s}{h}", [P, E], F32) for h in range(2)] for s in range(2)]
         for s in range(2):
@@ -71,22 +69,22 @@ def tile_list_twotables_bank_one_pagetwice_kernel(
         tb_rows = tb.rearrange("(p t) x -> t p x", t=PACK)
         tc_rows = tc2.rearrange("(p t) x -> t p x", t=PACK)
 
-        nc.sync.dma_start(xt_sb[:].bitcast(I32), xt_words[0].rearrange("p n t -> p (n t)").bitcast(I32))
         l1 = load_list("l1", offs)
-        load_plane(nc.sync, xt_plane, xt_scales)
         nc.sync.dma_start(w_sb[:].bitcast(I32), w_words[0].bitcast(I32))
-        nc.sync.dma_start(xo_sb[:].bitcast(I32), xo_words[0].rearrange("p n t -> p (n t)").bitcast(I32))
+        load_halves(xt_stage, xt_scales)
+        nc.sync.dma_start(xt_sb[:].bitcast(I32), xt_words[0].rearrange("p n t -> p (n t)").bitcast(I32))
         l2 = load_list("l2", offs2)
-        load_plane(nc.sync, xo_plane, xo_scales)
+        load_halves(xo_stage, xo_scales)
+        nc.sync.dma_start(xo_sb[:].bitcast(I32), xo_words[0].rearrange("p n t -> p (n t)").bitcast(I32))
         nc.sync.dma_start(w0_sb[:].bitcast(I32), w0_words[0].bitcast(I32))
-        load_halves(w_stage, w_scales)
-        load_halves(w0_stage, w0_scales)
+        load_halves(w_stage[:, :, 0:R], w_scales)
+        load_halves(w_stage[:, :, R : 2 * R], w0_scales)
         nc.sync.dma_start(tb_sb[0][:], tb_rows[0])
         nc.sync.dma_start(tc_sb[0][:], tc_rows[0])
-        l3 = load_list("l3", offs3)
-        l4 = load_list("l4", offs4)
         nc.sync.dma_start(tb_sb[1][:], tb_rows[1])
         l5 = load_list("l5", offs5)
+        l3 = load_list("l3", offs3)
+        l4 = load_list("l4", offs4)
         nc.sync.dma_start(tc_sb[1][:], tc_rows[1])
         for t in range(2, PACK):
             nc.sync.dma_start(tb_sb[t][:], tb_rows[t])
@@ -96,40 +94,51 @@ def tile_list_twotables_bank_one_pagetwice_kernel(
         l7 = load_list("l7", offs7)
         load_plane(nc.gpsimd, wb_plane, wb_scales)
 
-        def deal_weight(name, words, stage):
-            codes = tile(name + "_codes", [P, 2 * R], U8)
-            plane = tile(name + "_dealt", [P, R], U8)
+        def deal_codes(name, words):
+            codes = tile(name, [P, 2 * R], U8)
             nc.scalar.copy(
                 codes[:].bitcast(U16).rearrange("p (t c i) -> p c t i", t=PACK, i=8),
                 words[:].bitcast(U16).rearrange("p (c i t) -> p c t i", t=PACK, i=8),
             )
-            nc.vector.tensor_copy(stage[64:128, 0, :].bitcast(I32), stage[0:64, 1, :].bitcast(I32))
-            nc.vector.tensor_copy(
-                plane[:].rearrange("p (t c i) -> p c t i", t=PACK, i=16),
-                stage[:, 0, :].rearrange("p (c i t) -> p c t i", t=PACK, i=16),
-            )
-            return codes, plane
+            return codes
 
-        def pick(name, words, plane, lst):
-            gw = tile(name + "_gw", [P, J], U32)
+        def pick_scales(name, stage, lst):
+            plane = tile(name + "_plane", [P, T], U8)
+            for h in range(2):
+                nc.vector.tensor_copy(plane[64 * h : 64 * h + 64, :].bitcast(I32), stage[:, h, :].bitcast(I32))
             gs = tile(name + "_gs", [P, J], U8)
             nc.vector.tensor_copy(gs[:], plane[:].indirect(lst[:]))
-            nc.vector.tensor_copy(gw[:], words[:].indirect(lst[:]))
-            return gw, gs
+            return gs
 
-        xt_gw, xt_gs = pick("xt", xt_sb, xt_plane, l1)
-        w_codes, w_plane = deal_weight("w", w_sb, w_stage)
+        def pick_words(name, words, lst):
+            gw = tile(name + "_gw", [P, J], U32)
+            nc.vector.tensor_copy(gw[:], words[:].indirect(lst[:]))
+            return gw
+
+        xt_gs = pick_scales("xt", xt_stage, l1)
+        xt_gw = pick_words("xt", xt_sb, l1)
+        xo_gs = pick_scales("xo", xo_stage, l2)
+        xo_gw = pick_words("xo", xo_sb, l2)
+        nc.vector.tensor_copy(w_stage[64:128, 0, :].bitcast(I32), w_stage[0:64, 1, :].bitcast(I32))
+        by_slot = w_stage[:, 0, :].rearrange("p (s c i t) -> p t s c i", s=2, t=PACK, i=16)
+        first = tile("w_planes_first", [P, 2 * P], U8)
+        nc.vector.tensor_copy(first[:].rearrange("p (s c i) -> p s c i", s=2, i=16), by_slot[:, 0])
+        rest = tile("w_planes_rest", [P, (PACK - 1) * 2 * P], U8)
+        nc.vector.tensor_copy(
+            rest[:].rearrange("p (t s c i) -> p s c t i", s=2, t=PACK - 1, i=16),
+            by_slot[:, 1:PACK].rearrange("p t s c i -> p s c t i"),
+        )
+        planes = [first[:]] + [rest[:, 2 * P * t : 2 * P * (t + 1)] for t in range(PACK - 1)]
+        w_codes = deal_codes("w_codes", w_sb)
+        w0_codes = deal_codes("w0_codes", w0_sb)
         banks = [ps.tile([P, J], F32, name=f"acc{t}") for t in range(PACK)]
         for t in range(PACK):
             nc.tensor.matmul_mx(
-                banks[t][:], lhsT=w_codes[:, 2 * P * t : 2 * P * (t + 1)].bitcast(E2M1), lhsT_scale=w_plane[:, P * t : P * (t + 1)],
+                banks[t][:], lhsT=w_codes[:, 2 * P * t : 2 * P * (t + 1)].bitcast(E2M1), lhsT_scale=planes[t][:, 0:P],
                 rhs=xt_gw[:].bitcast(E5M2), rhs_scale=xt_gs[:], start=True, stop=False,
             )
-        xo_gw, xo_gs = pick("xo", xo_sb, xo_plane, l2)
-        w0_codes, w0_plane = deal_weight("w0", w0_sb, w0_stage)
-        for t in range(PACK):
             nc.tensor.matmul_mx(
-                banks[t][:], lhsT=w0_codes[:, 2 * P * t : 2 * P * (t + 1)].bitcast(E2M1), lhsT_scale=w0_plane[:, P * t : P * (t + 1)],
+                banks[t][:], lhsT=w0_codes[:, 2 * P * t : 2 * P * (t + 1)].bitcast(E2M1), lhsT_scale=planes[t][:, P : 2 * P],
                 rhs=xo_gw[:].bitcast(E4M3), rhs_scale=xo_gs[:], start=False, stop=True,
             )
 
@@ -138,22 +147,23 @@ def tile_list_twotables_bank_one_pagetwice_kernel(
         v = tile("v", [P, PACK, O], F32)
         m = tile("m", [P, PACK, O], F32)
         g = tile("g", [P, PACK, O], F32)
-        d = tile("d", [P, PACK, O], BF16)
         for t in range(PACK):
-            if t < 2:
-                nc.vector.tensor_copy(a_sb[t][:], banks[t][:])
-            else:
+            if t == 0:
                 nc.scalar.copy(a_sb[t][:], banks[t][:])
+            else:
+                nc.vector.tensor_copy(a_sb[t][:], banks[t][:])
+            nc.vector.tensor_copy(g[:, t, :], a_sb[t][:].indirect(l5[:]))
+        for t in range(PACK):
             nc.scalar.activation(u[:, t, :], tb_sb[t][:].indirect(l3[:]), COPY, scale=a_sb[t][:, 0:1])
             nc.scalar.activation(v[:, t, :], tc_sb[t][:].indirect(l4[:]), COPY, scale=a_sb[t][:, 128:129])
-            nc.vector.tensor_copy(g[:, t, :], a_sb[t][:].indirect(l5[:]))
             nc.vector.tensor_tensor(m[:, t, :], u[:, t, :], v[:, t, :], ALU.max)
-            nc.vector.tensor_tensor(d[:, t, :], m[:, t, :], g[:, t, :], ALU.subtract)
 
         hid = tile("hid", [P, O * PACK], BF16)
-        nc.vector.tensor_copy(
+        nc.vector.tensor_tensor(
             hid[:].rearrange("p (c i t) -> p c t i", t=PACK, i=4),
-            d[:].rearrange("p t (c i) -> p c t i", i=4),
+            m[:].rearrange("p t (c i) -> p c t i", i=4),
+            g[:].rearrange("p t (c i) -> p c t i", i=4),
+            ALU.subtract,
         )
         hid_codes = tile("hid_codes", [P, O], U32)
         hid_plane = tile("hid_plane", [P, O], U8)
@@ -173,7 +183,7 @@ def tile_list_twotables_bank_one_pagetwice_kernel(
         for h in range(2):
             nc.vector.tensor_copy(pages[0][h][:].indirect(l6[:]), p_sb[h][:])
             nc.scalar.activation(pages[1][h][:].indirect(l7[:]), p_sb[h][:], COPY)
-        for h in range(2):
-            y = tile(f"y{h}", [P, E], F32)
-            nc.vector.tensor_tensor(y[:], pages[0][h][:], pages[1][h][:], ALU.add)
-            nc.sync.dma_start(out[P * h : P * (h + 1), :], y[:])
+        for h, c0, c1, queue in ((0, 0, E, nc.sync), (1, 0, E // 2, nc.scalar), (1, E // 2, E, nc.sync)):
+            y = tile(f"y{h}{c0}", [P, c1 - c0], F32)
+            nc.vector.tensor_tensor(y[:], pages[0][h][:, c0:c1], pages[1][h][:, c0:c1], ALU.add)
+            queue.dma_start(out[P * h : P * (h + 1), c0:c1], y[:])

@@ -17,6 +17,7 @@ COPY = mybir.ActivationFunctionType.Copy
 P = 128
 PACK = 4
 T, J, R, X, O, N, E = 1024, 256, 512, 512, 128, 256, 512
+H = J // 2
 FLOPS = 2 * (2 * 512 * R * J + R * N * O)
 
 
@@ -27,6 +28,7 @@ def tile_list_twotables_bank_one_pagetwice_kernel(
     nc = tc.nc
     with ExitStack() as ctx:
         sb = ctx.enter_context(tc.tile_pool(name="sb", bufs=1))
+        reused = ctx.enter_context(tc.tile_pool(name="reused", bufs=1))
         ps = ctx.enter_context(tc.psum_pool(name="ps", bufs=1))
 
         def tile(name, shape, dtype):
@@ -37,23 +39,21 @@ def tile_list_twotables_bank_one_pagetwice_kernel(
             nc.sync.dma_start(t[:], src)
             return t
 
-        def load_plane(queue, plane, src):
-            for q in range(4):
-                queue.dma_start(plane[32 * q : 32 * q + 4, :].bitcast(I32), src[0, 4 * q : 4 * q + 4, :].bitcast(I32))
-
         def load_halves(stage, src):
             rows = src[0].rearrange("(h q r) n -> q r h n", h=2, q=2, r=4)
             for q in range(2):
                 nc.sync.dma_start(stage[32 * q : 32 * q + 4].bitcast(I32), rows[q].bitcast(I32))
 
-        xt_stage = tile("xt_stage", [64, 2, T], U8)
+        xt_stage = tile("xt_stage", [4, 4, T], U8)
+        xt_plane = tile("xt_plane", [P, T], U8)
         xo_stage = tile("xo_stage", [64, 2, T], U8)
-        w_stage = tile("w_stage", [P, 2, 2 * R], U8)
+        xo_plane = tile("xo_plane", [P, T], U8)
+        w_stage = reused.tile([P, 2, 2 * R], U8, name="w_stage", align_bytes=64, offset=0)
         wb_plane = tile("wb_plane", [P, N], U8)
-        nc.vector.memset(xt_stage[:].bitcast(I32), 0)
         nc.vector.memset(xo_stage[:].bitcast(I32), 0)
         nc.vector.memset(w_stage[0:64].bitcast(I32), 0)
         nc.vector.memset(wb_plane[:].bitcast(I32), 0)
+        nc.vector.memset(xt_plane[:].bitcast(I32), 0)
         pages = [[tile(f"page{s}{h}", [P, E], F32) for h in range(2)] for s in range(2)]
         for s in range(2):
             for h in range(2):
@@ -69,30 +69,30 @@ def tile_list_twotables_bank_one_pagetwice_kernel(
         tb_rows = tb.rearrange("(p t) x -> t p x", t=PACK)
         tc_rows = tc2.rearrange("(p t) x -> t p x", t=PACK)
 
+        nc.sync.dma_start(xt_stage[:].bitcast(I32), xt_scales[0].rearrange("(q r) n -> r q n", r=4).bitcast(I32))
         l1 = load_list("l1", offs)
-        nc.sync.dma_start(w_sb[:].bitcast(I32), w_words[0].bitcast(I32))
-        load_halves(xt_stage, xt_scales)
         nc.sync.dma_start(xt_sb[:].bitcast(I32), xt_words[0].rearrange("p n t -> p (n t)").bitcast(I32))
         l2 = load_list("l2", offs2)
         load_halves(xo_stage, xo_scales)
+        nc.sync.dma_start(w_sb[:].bitcast(I32), w_words[0].bitcast(I32))
         nc.sync.dma_start(xo_sb[:].bitcast(I32), xo_words[0].rearrange("p n t -> p (n t)").bitcast(I32))
-        nc.sync.dma_start(w0_sb[:].bitcast(I32), w0_words[0].bitcast(I32))
         load_halves(w_stage[:, :, 0:R], w_scales)
+        nc.sync.dma_start(w0_sb[:].bitcast(I32), w0_words[0].bitcast(I32))
         load_halves(w_stage[:, :, R : 2 * R], w0_scales)
         nc.sync.dma_start(tb_sb[0][:], tb_rows[0])
-        nc.sync.dma_start(tc_sb[0][:], tc_rows[0])
         nc.sync.dma_start(tb_sb[1][:], tb_rows[1])
-        l5 = load_list("l5", offs5)
         l3 = load_list("l3", offs3)
+        nc.sync.dma_start(tb_sb[2][:], tb_rows[2])
+        nc.sync.dma_start(tb_sb[3][:], tb_rows[3])
+        l5 = load_list("l5", offs5)
         l4 = load_list("l4", offs4)
-        nc.sync.dma_start(tc_sb[1][:], tc_rows[1])
-        for t in range(2, PACK):
-            nc.sync.dma_start(tb_sb[t][:], tb_rows[t])
+        for t in range(PACK):
             nc.sync.dma_start(tc_sb[t][:], tc_rows[t])
+        for q in range(4):
+            nc.gpsimd.dma_start(wb_plane[32 * q : 32 * q + 4, :].bitcast(I32), wb_scales[0, 4 * q : 4 * q + 4, :].bitcast(I32))
         nc.sync.dma_start(wb_sb[:].bitcast(I32), wb_words[0].bitcast(I32))
         l6 = load_list("l6", offs6)
         l7 = load_list("l7", offs7)
-        load_plane(nc.gpsimd, wb_plane, wb_scales)
 
         def deal_codes(name, words):
             codes = tile(name, [P, 2 * R], U8)
@@ -102,23 +102,19 @@ def tile_list_twotables_bank_one_pagetwice_kernel(
             )
             return codes
 
-        def pick_scales(name, stage, lst):
-            plane = tile(name + "_plane", [P, T], U8)
-            for h in range(2):
-                nc.vector.tensor_copy(plane[64 * h : 64 * h + 64, :].bitcast(I32), stage[:, h, :].bitcast(I32))
-            gs = tile(name + "_gs", [P, J], U8)
-            nc.vector.tensor_copy(gs[:], plane[:].indirect(lst[:]))
-            return gs
+        for q in range(4):
+            nc.vector.tensor_copy(xt_plane[32 * q : 32 * q + 4, :].bitcast(I32), xt_stage[:, q, :].bitcast(I32))
+        xt_gs = tile("xt_gs", [P, J], U8)
+        xt_gw = tile("xt_gw", [P, J], U32)
+        nc.vector.tensor_copy(xt_gs[:], xt_plane[:].indirect(l1[:]))
+        nc.vector.tensor_copy(xt_gw[:], xt_sb[:].indirect(l1[:]))
+        for h in range(2):
+            nc.vector.tensor_copy(xo_plane[64 * h : 64 * h + 64, :].bitcast(I32), xo_stage[:, h, :].bitcast(I32))
+        xo_gs = [tile("xo_gs0", [P, H], U8)]
+        xo_gw = [tile("xo_gw0", [P, H], U32)]
+        nc.vector.tensor_copy(xo_gs[0][:], xo_plane[:].indirect(l2[:, 0 : H // 16]))
+        nc.vector.tensor_copy(xo_gw[0][:], xo_sb[:].indirect(l2[:, 0 : H // 16]))
 
-        def pick_words(name, words, lst):
-            gw = tile(name + "_gw", [P, J], U32)
-            nc.vector.tensor_copy(gw[:], words[:].indirect(lst[:]))
-            return gw
-
-        xt_gs = pick_scales("xt", xt_stage, l1)
-        xt_gw = pick_words("xt", xt_sb, l1)
-        xo_gs = pick_scales("xo", xo_stage, l2)
-        xo_gw = pick_words("xo", xo_sb, l2)
         nc.vector.tensor_copy(w_stage[64:128, 0, :].bitcast(I32), w_stage[0:64, 1, :].bitcast(I32))
         by_slot = w_stage[:, 0, :].rearrange("p (s c i t) -> p t s c i", s=2, t=PACK, i=16)
         first = tile("w_planes_first", [P, 2 * P], U8)
@@ -129,49 +125,64 @@ def tile_list_twotables_bank_one_pagetwice_kernel(
             by_slot[:, 1:PACK].rearrange("p t s c i -> p s c t i"),
         )
         planes = [first[:]] + [rest[:, 2 * P * t : 2 * P * (t + 1)] for t in range(PACK - 1)]
+        xo_gs.append(reused.tile([P, H], U8, name="xo_gs1", align_bytes=64, offset=0))
+        xo_gw.append(reused.tile([P, H], U32, name="xo_gw1", align_bytes=64, offset=H))
+        nc.vector.tensor_copy(xo_gs[1][:], xo_plane[:].indirect(l2[:, H // 16 : J // 16]))
+        nc.vector.tensor_copy(xo_gw[1][:], xo_sb[:].indirect(l2[:, H // 16 : J // 16]))
         w_codes = deal_codes("w_codes", w_sb)
         w0_codes = deal_codes("w0_codes", w0_sb)
-        banks = [ps.tile([P, J], F32, name=f"acc{t}") for t in range(PACK)]
-        for t in range(PACK):
-            nc.tensor.matmul_mx(
-                banks[t][:], lhsT=w_codes[:, 2 * P * t : 2 * P * (t + 1)].bitcast(E2M1), lhsT_scale=planes[t][:, 0:P],
-                rhs=xt_gw[:].bitcast(E5M2), rhs_scale=xt_gs[:], start=True, stop=False,
-            )
-            nc.tensor.matmul_mx(
-                banks[t][:], lhsT=w0_codes[:, 2 * P * t : 2 * P * (t + 1)].bitcast(E2M1), lhsT_scale=planes[t][:, P : 2 * P],
-                rhs=xo_gw[:].bitcast(E4M3), rhs_scale=xo_gs[:], start=False, stop=True,
-            )
 
         a_sb = [tile(f"a{t}", [P, J], F32) for t in range(PACK)]
         u = tile("u", [P, PACK, O], F32)
         v = tile("v", [P, PACK, O], F32)
         m = tile("m", [P, PACK, O], F32)
         g = tile("g", [P, PACK, O], F32)
+        for half in range(2):
+            cols = slice(H * half, H * (half + 1))
+            for t in range(PACK):
+                acc = ps.tile([P, H], F32, name=f"acc{half}{t}", tag=f"bank{half}{t}")
+                nc.tensor.matmul_mx(
+                    acc[:], lhsT=w_codes[:, 2 * P * t : 2 * P * (t + 1)].bitcast(E2M1), lhsT_scale=planes[t][:, 0:P],
+                    rhs=xt_gw[:, cols].bitcast(E5M2), rhs_scale=xt_gs[:, cols], start=True, stop=False,
+                )
+                nc.tensor.matmul_mx(
+                    acc[:], lhsT=w0_codes[:, 2 * P * t : 2 * P * (t + 1)].bitcast(E2M1), lhsT_scale=planes[t][:, P : 2 * P],
+                    rhs=xo_gw[half][:].bitcast(E4M3), rhs_scale=xo_gs[half][:], start=False, stop=True,
+                )
+                if half == 0:
+                    nc.scalar.copy(a_sb[t][:, cols], acc[:])
+                    nc.scalar.activation(u[:, t, :], tb_sb[t][:].indirect(l3[:]), COPY, scale=a_sb[t][:, 0:1])
+                else:
+                    nc.vector.tensor_copy(a_sb[t][:, cols], acc[:])
         for t in range(PACK):
-            if t == 0:
-                nc.scalar.copy(a_sb[t][:], banks[t][:])
-            else:
-                nc.vector.tensor_copy(a_sb[t][:], banks[t][:])
             nc.vector.tensor_copy(g[:, t, :], a_sb[t][:].indirect(l5[:]))
-        for t in range(PACK):
-            nc.scalar.activation(u[:, t, :], tb_sb[t][:].indirect(l3[:]), COPY, scale=a_sb[t][:, 0:1])
-            nc.scalar.activation(v[:, t, :], tc_sb[t][:].indirect(l4[:]), COPY, scale=a_sb[t][:, 128:129])
+        last = PACK - 1
+        halves = [slice(0, O // 2), slice(O // 2, O)]
+        for t in range(last):
+            nc.scalar.activation(v[:, t, :], tc_sb[t][:].indirect(l4[:]), COPY, scale=a_sb[t][:, H : H + 1])
             nc.vector.tensor_tensor(m[:, t, :], u[:, t, :], v[:, t, :], ALU.max)
-
-        hid = tile("hid", [P, O * PACK], BF16)
-        nc.vector.tensor_tensor(
-            hid[:].rearrange("p (c i t) -> p c t i", t=PACK, i=4),
-            m[:].rearrange("p t (c i) -> p c t i", i=4),
-            g[:].rearrange("p t (c i) -> p c t i", i=4),
-            ALU.subtract,
-        )
+        for c in halves:
+            nc.scalar.activation(
+                v[:, last, c], tc_sb[last][:].indirect(l4[:, c.start // 16 : c.stop // 16]), COPY, scale=a_sb[last][:, H : H + 1]
+            )
+        for c in halves:
+            nc.vector.tensor_tensor(m[:, last, c], u[:, last, c], v[:, last, c], ALU.max)
+        hid = [tile(f"hid{i}", [P, O // 2 * PACK], BF16) for i in range(2)]
+        for i, c in enumerate(halves):
+            nc.vector.tensor_tensor(
+                hid[i][:].rearrange("p (c i t) -> p c t i", t=PACK, i=4),
+                m[:, :, c].rearrange("p t (c i) -> p c t i", i=4),
+                g[:, :, c].rearrange("p t (c i) -> p c t i", i=4),
+                ALU.subtract,
+            )
         hid_codes = tile("hid_codes", [P, O], U32)
         hid_plane = tile("hid_plane", [P, O], U8)
-        nc.vector.quantize_mx(hid_codes[:].bitcast(E4M3), hid_plane[:], hid[:])
+        for i, c in enumerate(halves):
+            nc.vector.quantize_mx(hid_codes[:, c].bitcast(E4M3), hid_plane[:, c], hid[i][:])
 
         p_sb = [tile(f"p{h}", [P, O], F32) for h in range(2)]
         for h in range(2):
-            acc = ps.tile([P, O], F32, name=f"pacc{h}")
+            acc = ps.tile([P, O], F32, name=f"pacc{h}", tag=f"bank0{h}")
             nc.tensor.matmul_mx(
                 acc[:], lhsT=wb_sb[:, 2 * P * h : 2 * P * (h + 1)].bitcast(E2M1), lhsT_scale=wb_plane[:, P * h : P * (h + 1)],
                 rhs=hid_codes[:].bitcast(E4M3), rhs_scale=hid_plane[:], start=True, stop=True,

from contextlib import ExitStack

import concourse.mybir as mybir

F32 = mybir.dt.float32
BF16 = mybir.dt.bfloat16
I32 = mybir.dt.int32
U32 = mybir.dt.uint32
U16 = mybir.dt.uint16
U8 = mybir.dt.uint8
E4M3 = mybir.dt.float8_e4m3fn_x4
E5M2 = mybir.dt.float8_e5m2_x4
E2M1 = mybir.dt.float4_e2m1fn_x4
ALU = mybir.AluOpType
COPY = mybir.ActivationFunctionType.Copy

P = 128
PACK = 4
T, J, R, X, O, N, E = 1024, 256, 512, 512, 128, 256, 512
H = J // 2
FLOPS = 2 * (2 * 512 * R * J + R * N * O)


def tile_list_twotables_bank_one_pagetwice_kernel(
    tc, xt_words, xt_scales, xo_words, xo_scales, w_words, w_scales, w0_words, w0_scales,
    tb, tc2, wb_words, wb_scales, offs, offs2, offs3, offs4, offs5, offs6, offs7, out,
):
    nc = tc.nc
    with ExitStack() as ctx:
        sb = ctx.enter_context(tc.tile_pool(name="sb", bufs=1))
        reused = ctx.enter_context(tc.tile_pool(name="reused", bufs=1))
        ps = ctx.enter_context(tc.psum_pool(name="ps", bufs=1))

        def tile(name, shape, dtype):
            return sb.tile(shape, dtype, name=name, align_bytes=64)

        def load_list(name, src):
            t = tile(name, list(src.shape), U16)
            nc.sync.dma_start(t[:], src)
            return t

        def load_halves(stage, src):
            rows = src[0].rearrange("(h q r) n -> q r h n", h=2, q=2, r=4)
            for q in range(2):
                nc.sync.dma_start(stage[32 * q : 32 * q + 4].bitcast(I32), rows[q].bitcast(I32))

        xt_stage = tile("xt_stage", [4, 4, T], U8)
        xt_plane = tile("xt_plane", [P, T], U8)
        xo_stage = tile("xo_stage", [64, 2, T], U8)
        xo_plane = tile("xo_plane", [P, T], U8)
        w_stage = reused.tile([P, 2, 2 * R], U8, name="w_stage", align_bytes=64, offset=0)
        wb_plane = tile("wb_plane", [P, N], U8)
        nc.vector.memset(xo_stage[:].bitcast(I32), 0)
        nc.vector.memset(w_stage[0:64].bitcast(I32), 0)
        nc.vector.memset(wb_plane[:].bitcast(I32), 0)
        nc.vector.memset(xt_plane[:].bitcast(I32), 0)
        pages = [[tile(f"page{s}{h}", [P, E], F32) for h in range(2)] for s in range(2)]
        for s in range(2):
            for h in range(2):
                nc.vector.memset(pages[s][h][:], 0.0)

        xt_sb = tile("xt_sb", [P, T], U32)
        xo_sb = tile("xo_sb", [P, T], U32)
        w_sb = tile("w_sb", [P, 2 * R], U8)
        w0_sb = tile("w0_sb", [P, 2 * R], U8)
        wb_sb = tile("wb_sb", [P, 2 * N], U8)
        tb_sb = [tile(f"tb{t}", [P, X], F32) for t in range(PACK)]
        tc_sb = [tile(f"tc{t}", [P, X], F32) for t in range(PACK)]
        tb_rows = tb.rearrange("(p t) x -> t p x", t=PACK)
        tc_rows = tc2.rearrange("(p t) x -> t p x", t=PACK)

        nc.sync.dma_start(xt_stage[:].bitcast(I32), xt_scales[0].rearrange("(q r) n -> r q n", r=4).bitcast(I32))
        l1 = load_list("l1", offs)
        nc.sync.dma_start(xt_sb[:].bitcast(I32), xt_words[0].rearrange("p n t -> p (n t)").bitcast(I32))
        l2 = load_list("l2", offs2)
        load_halves(xo_stage, xo_scales)
        nc.sync.dma_start(w_sb[:].bitcast(I32), w_words[0].bitcast(I32))
        nc.sync.dma_start(xo_sb[:].bitcast(I32), xo_words[0].rearrange("p n t -> p (n t)").bitcast(I32))
        load_halves(w_stage[:, :, 0:R], w_scales)
        nc.sync.dma_start(w0_sb[:].bitcast(I32), w0_words[0].bitcast(I32))
        load_halves(w_stage[:, :, R : 2 * R], w0_scales)
        nc.sync.dma_start(tb_sb[0][:], tb_rows[0])
        nc.sync.dma_start(tb_sb[1][:], tb_rows[1])
        l3 = load_list("l3", offs3)
        nc.sync.dma_start(tb_sb[2][:], tb_rows[2])
        nc.sync.dma_start(tb_sb[3][:], tb_rows[3])
        l5 = load_list("l5", offs5)
        l4 = load_list("l4", offs4)
        for t in range(PACK):
            nc.sync.dma_start(tc_sb[t][:], tc_rows[t])
        for q in range(4):
            nc.gpsimd.dma_start(wb_plane[32 * q : 32 * q + 4, :].bitcast(I32), wb_scales[0, 4 * q : 4 * q + 4, :].bitcast(I32))
        nc.sync.dma_start(wb_sb[:].bitcast(I32), wb_words[0].bitcast(I32))
        l6 = load_list("l6", offs6)
        l7 = load_list("l7", offs7)

        def deal_codes(name, words):
            codes = tile(name, [P, 2 * R], U8)
            nc.scalar.copy(
                codes[:].bitcast(U16).rearrange("p (t c i) -> p c t i", t=PACK, i=8),
                words[:].bitcast(U16).rearrange("p (c i t) -> p c t i", t=PACK, i=8),
            )
            return codes

        for q in range(4):
            nc.vector.tensor_copy(xt_plane[32 * q : 32 * q + 4, :].bitcast(I32), xt_stage[:, q, :].bitcast(I32))
        xt_gs = tile("xt_gs", [P, J], U8)
        xt_gw = tile("xt_gw", [P, J], U32)
        nc.vector.tensor_copy(xt_gs[:], xt_plane[:].indirect(l1[:]))
        nc.vector.tensor_copy(xt_gw[:], xt_sb[:].indirect(l1[:]))
        for h in range(2):
            nc.vector.tensor_copy(xo_plane[64 * h : 64 * h + 64, :].bitcast(I32), xo_stage[:, h, :].bitcast(I32))
        xo_gs = [tile("xo_gs0", [P, H], U8)]
        xo_gw = [tile("xo_gw0", [P, H], U32)]
        nc.vector.tensor_copy(xo_gs[0][:], xo_plane[:].indirect(l2[:, 0 : H // 16]))
        nc.vector.tensor_copy(xo_gw[0][:], xo_sb[:].indirect(l2[:, 0 : H // 16]))

        nc.vector.tensor_copy(w_stage[64:128, 0, :].bitcast(I32), w_stage[0:64, 1, :].bitcast(I32))
        by_slot = w_stage[:, 0, :].rearrange("p (s c i t) -> p t s c i", s=2, t=PACK, i=16)
        first = tile("w_planes_first", [P, 2 * P], U8)
        nc.vector.tensor_copy(first[:].rearrange("p (s c i) -> p s c i", s=2, i=16), by_slot[:, 0])
        rest = tile("w_planes_rest", [P, (PACK - 1) * 2 * P], U8)
        nc.vector.tensor_copy(
            rest[:].rearrange("p (t s c i) -> p s c t i", s=2, t=PACK - 1, i=16),
            by_slot[:, 1:PACK].rearrange("p t s c i -> p s c t i"),
        )
        planes = [first[:]] + [rest[:, 2 * P * t : 2 * P * (t + 1)] for t in range(PACK - 1)]
        xo_gs.append(reused.tile([P, H], U8, name="xo_gs1", align_bytes=64, offset=0))
        xo_gw.append(reused.tile([P, H], U32, name="xo_gw1", align_bytes=64, offset=H))
        nc.vector.tensor_copy(xo_gs[1][:], xo_plane[:].indirect(l2[:, H // 16 : J // 16]))
        nc.vector.tensor_copy(xo_gw[1][:], xo_sb[:].indirect(l2[:, H // 16 : J // 16]))
        w_codes = deal_codes("w_codes", w_sb)
        w0_codes = deal_codes("w0_codes", w0_sb)

        a_sb = [tile(f"a{t}", [P, J], F32) for t in range(PACK)]
        u = tile("u", [P, PACK, O], F32)
        v = tile("v", [P, PACK, O], F32)
        m = tile("m", [P, PACK, O], F32)
        g = tile("g", [P, PACK, O], F32)
        for half in range(2):
            cols = slice(H * half, H * (half + 1))
            for t in range(PACK):
                acc = ps.tile([P, H], F32, name=f"acc{half}{t}", tag=f"bank{half}{t}")
                nc.tensor.matmul_mx(
                    acc[:], lhsT=w_codes[:, 2 * P * t : 2 * P * (t + 1)].bitcast(E2M1), lhsT_scale=planes[t][:, 0:P],
                    rhs=xt_gw[:, cols].bitcast(E5M2), rhs_scale=xt_gs[:, cols], start=True, stop=False,
                )
                nc.tensor.matmul_mx(
                    acc[:], lhsT=w0_codes[:, 2 * P * t : 2 * P * (t + 1)].bitcast(E2M1), lhsT_scale=planes[t][:, P : 2 * P],
                    rhs=xo_gw[half][:].bitcast(E4M3), rhs_scale=xo_gs[half][:], start=False, stop=True,
                )
                if half == 0:
                    nc.scalar.copy(a_sb[t][:, cols], acc[:])
                    nc.scalar.activation(u[:, t, :], tb_sb[t][:].indirect(l3[:]), COPY, scale=a_sb[t][:, 0:1])
                else:
                    nc.vector.tensor_copy(a_sb[t][:, cols], acc[:])
        for t in range(PACK):
            nc.vector.tensor_copy(g[:, t, :], a_sb[t][:].indirect(l5[:]))
        last = PACK - 1
        halves = [slice(0, O // 2), slice(O // 2, O)]
        for t in range(last):
            nc.scalar.activation(v[:, t, :], tc_sb[t][:].indirect(l4[:]), COPY, scale=a_sb[t][:, H : H + 1])
            nc.vector.tensor_tensor(m[:, t, :], u[:, t, :], v[:, t, :], ALU.max)
        for c in halves:
            nc.scalar.activation(
                v[:, last, c], tc_sb[last][:].indirect(l4[:, c.start // 16 : c.stop // 16]), COPY, scale=a_sb[last][:, H : H + 1]
            )
        for c in halves:
            nc.vector.tensor_tensor(m[:, last, c], u[:, last, c], v[:, last, c], ALU.max)
        hid = [tile(f"hid{i}", [P, O // 2 * PACK], BF16) for i in range(2)]
        for i, c in enumerate(halves):
            nc.vector.tensor_tensor(
                hid[i][:].rearrange("p (c i t) -> p c t i", t=PACK, i=4),
                m[:, :, c].rearrange("p t (c i) -> p c t i", i=4),
                g[:, :, c].rearrange("p t (c i) -> p c t i", i=4),
                ALU.subtract,
            )
        hid_codes = tile("hid_codes", [P, O], U32)
        hid_plane = tile("hid_plane", [P, O], U8)
        for i, c in enumerate(halves):
            nc.vector.quantize_mx(hid_codes[:, c].bitcast(E4M3), hid_plane[:, c], hid[i][:])

        p_sb = [tile(f"p{h}", [P, O], F32) for h in range(2)]
        for h in range(2):
            acc = ps.tile([P, O], F32, name=f"pacc{h}", tag=f"bank0{h}")
            nc.tensor.matmul_mx(
                acc[:], lhsT=wb_sb[:, 2 * P * h : 2 * P * (h + 1)].bitcast(E2M1), lhsT_scale=wb_plane[:, P * h : P * (h + 1)],
                rhs=hid_codes[:].bitcast(E4M3), rhs_scale=hid_plane[:], start=True, stop=True,
            )
            if h == 0:
                nc.vector.tensor_copy(p_sb[h][:], acc[:])
            else:
                nc.scalar.copy(p_sb[h][:], acc[:])
        for h in range(2):
            nc.vector.tensor_copy(pages[0][h][:].indirect(l6[:]), p_sb[h][:])
            nc.scalar.activation(pages[1][h][:].indirect(l7[:]), p_sb[h][:], COPY)
        for h, c0, c1, queue in ((0, 0, E, nc.sync), (1, 0, E // 2, nc.scalar), (1, E // 2, E, nc.sync)):
            y = tile(f"y{h}{c0}", [P, c1 - c0], F32)
            nc.vector.tensor_tensor(y[:], pages[0][h][:, c0:c1], pages[1][h][:, c0:c1], ALU.add)
            queue.dma_start(out[P * h : P * (h + 1), c0:c1], y[:])
